import numpy as np
import ml_dtypes


def mxq(x, axis, fmt="e4m3"):
    dtype, down = {"e4m3": (ml_dtypes.float8_e4m3fn, 7), "e5m2": (ml_dtypes.float8_e5m2, 14)}[fmt]
    v = np.moveaxis(np.asarray(x, np.float32).astype(ml_dtypes.bfloat16).astype(np.float64), axis, -1)
    blocks = v.reshape(v.shape[:-1] + (-1, 32))
    amax = np.abs(blocks).max(-1, keepdims=True)
    byte = np.maximum(np.where(amax > 0, np.frexp(amax)[1] - 1 + 127, 0) - down, 1)
    scale = np.exp2(byte - 127.0)
    codes = (blocks / scale).astype(np.float32).astype(dtype).astype(np.float64)
    return np.moveaxis((codes * scale).reshape(v.shape), -1, axis)


WIDE = False


def mx_kscale(k):
    if not WIDE:
        return np.ones(k)
    levels = np.array([10, -10, 5, -5, 0])
    if k % 512:
        return np.exp2(np.random.permutation(np.resize(levels, k // 32))).repeat(32)
    a = np.empty((k // 512, 16))
    for p in range(k // 512):
        a[p, :8] = np.random.permutation(np.resize(levels, 8))
        for g in range(8):
            far = levels[np.abs(levels - a[p, g]) >= 10]
            a[p, g + 8] = far[np.random.randint(len(far))]
    return np.exp2(a.ravel()).repeat(32)


def f64(x):
    return np.asarray(x).astype(np.float64)


def striped(idx):
    return np.tile(idx.reshape(-1, 16).T, (8, 1)).astype(np.uint16)


def unstriped(offs):
    return offs[:16].T.reshape(-1).astype(np.int64)


E2M1 = np.array([0.0, 0.5, 1.0, 1.5, 2.0, 3.0, 4.0, 6.0, -0.0, -0.5, -1.0, -1.5, -2.0, -3.0, -4.0, -6.0])


def pack_weight(w, fmt):
    k, n = w.shape
    w = f64(np.asarray(w, np.float32).astype(ml_dtypes.bfloat16)).reshape(k // 32, 32, n)
    amax = np.abs(w).max(1)
    if fmt == "e4m3":
        byte = np.frexp(amax)[1] - 1 + 127 - 7
    else:
        mant, ex = np.frexp(amax / 6.0)
        byte = np.where(mant > 0.5, ex, ex - 1) + 127
    byte = np.clip(np.where(amax > 0, byte, 1), 1, 254)
    scaled = (w * np.exp2(127.0 - byte)[:, None, :]).reshape(k, n).astype(np.float32)
    by_word = np.ascontiguousarray(scaled.reshape(k // 512, 128, 4, n).transpose(0, 1, 3, 2))
    if fmt == "e4m3":
        words = by_word.astype(ml_dtypes.float8_e4m3fn).view(np.uint8)
    else:
        c = by_word.astype(ml_dtypes.float4_e2m1fn).view(np.uint8) & 0xF
        words = (c[..., 0::2] | (c[..., 1::2] << 4)).reshape(k // 512, 128, 2 * n)
    return np.ascontiguousarray(words), np.ascontiguousarray(byte.astype(np.uint8).reshape(k // 512, 16, n))


def unpack_weight(words, scales, fmt):
    g, _, n = scales.shape
    words = np.ascontiguousarray(words).reshape(g, 128, n, -1)
    if fmt == "e4m3":
        vals = words.view(ml_dtypes.float8_e4m3fn).astype(np.float64)
    else:
        nib = np.empty((g, 128, n, 4), np.uint8)
        nib[..., 0::2] = words & 0xF
        nib[..., 1::2] = words >> 4
        vals = E2M1[nib]
    vals = vals * np.repeat(np.exp2(scales.astype(np.float64) - 127.0), 8, axis=1)[..., None]
    return vals.transpose(0, 1, 3, 2).reshape(g * 512, n)


def relu(v):
    return np.maximum(v, 0.0)


K, T, E, C, H, N = 1024, 1536, 12, 128, 512, 128
TOP = 4
PAD = 64


def by_expert(wq, xq):
    return np.concatenate([wq[e].T @ xq[:, e * C:(e + 1) * C] for e in range(E)], axis=1)


def setup_inputs():
    n = np.random.standard_normal
    s = mx_kscale(K)[:, None]
    u = mx_kscale(H)
    slot_token = np.empty(E * C, np.int64); pos = np.tile(E * C + np.arange(T) % PAD, (TOP, 1)); taken = np.zeros(T, np.int64)
    liked = np.random.randn(T)
    for e in np.random.permutation(E):
        free = np.flatnonzero(taken < TOP); pick = np.random.permutation(free[np.argsort(-(liked[free] + np.random.gumbel(size=free.size)))[:C]]); slot_token[e * C:(e + 1) * C] = pick
        pos[taken[pick], pick] = e * C + np.arange(C); taken[pick] += 1
    g = np.random.uniform(0.2, 0.8, (TOP, T))
    x = pack_weight(n((K, T)) * s, "e4m3")
    return {
        "x_words": x[0],
        "x_scales": x[1],
        "w1": (n((E, K, H)) / np.sqrt(K) / s[None] * u[None, None, :]).astype(np.float32),
        "w2": (n((E, H, N)) / np.sqrt(H) / u[None, :, None]).astype(np.float32),
        "gate": np.stack([np.tile(r, (N, 1)) for r in g]).astype(np.float32),
        "offs": striped(slot_token),
        "pos1": striped(pos[0]),
        "pos2": striped(pos[1]),
        "pos3": striped(pos[2]),
        "pos4": striped(pos[3]),
    }


def reference(x_words, x_scales, w1, w2, gate, offs, pos1, pos2, pos3, pos4):
    idx = unstriped(offs)
    xq = unpack_weight(x_words, x_scales, "e4m3")[:, idx]
    h = relu(by_expert(mxq(f64(w1), 1, "e4m3"), xq))
    y = by_expert(mxq(f64(w2), 1, "e4m3"), mxq(h, 0, "e4m3"))
    y = np.concatenate([y, np.zeros((N, PAD))], axis=1)
    return sum(f64(gate[r]) * y[:, unstriped(p)] for r, p in enumerate((pos1, pos2, pos3, pos4)))

@@ -1,0 +1,239 @@
+from contextlib import ExitStack
+
+import concourse.mybir as mybir
+from concourse.masks import make_identity
+
+K, T, E, C, H, N = 1024, 1536, 12, 128, 512, 128
+TOP = 4
+PAD = 64
+SLOTS = E * C
+
+FLOPS = 2 * SLOTS * (K * H + H * N)
+
+F32 = mybir.dt.float32
+BF16 = mybir.dt.bfloat16
+I32 = mybir.dt.int32
+U32 = mybir.dt.uint32
+U16 = mybir.dt.uint16
+U8 = mybir.dt.uint8
+FP8X4 = mybir.dt.float8_e4m3fn_x4
+RELU = mybir.ActivationFunctionType.Relu
+COPY = mybir.ActivationFunctionType.Copy
+
+P = 128
+PACK = 4
+K_PASS = P * PACK
+PASSES = K // K_PASS
+PER_COLUMN = 16
+GATHER = 256
+BLOCKS = T // P
+W2_EARLY = {1: (0, 2), 3: (2, 2), 5: (4, 2)}
+LAG = 2
+W2_LATE = ((6, 2), (8, 2), (10, 1), (11, 1))
+TOKEN_CHUNKS = (512, 512, 256, 256)
+
+
+def tile_moe_ecr_mlp_relu_kernel(
+    tc, x_words, x_scales, w1, w2, gate, offs, pos1, pos2, pos3, pos4, out
+):
+    nc = tc.nc
+    with ExitStack() as ctx:
+        lists = ctx.enter_context(tc.tile_pool(name="lists", bufs=1))
+        keep = ctx.enter_context(tc.tile_pool(name="keep", bufs=1))
+        ring = ctx.enter_context(tc.tile_pool(name="ring", bufs=1))
+        psum = ctx.enter_context(tc.psum_pool(name="psum", bufs=1))
+
+        def load_list(source, name):
+            tile = lists.tile([P, T // PER_COLUMN], U16, name=name)
+            nc.sync.dma_start(tile[:], source)
+            return tile
+
+        def load_w1(e, o):
+            raw = ring.tile([P, PACK, H], F32, name="w1_raw", bufs=10, align_bytes=64)
+            rows = w1[e, o * K_PASS:(o + 1) * K_PASS, :]
+            nc.sync.dma_start(raw[:], rows.rearrange("(p j) h -> p j h", j=PACK))
+            return raw
+
+        def load_w2(first, count):
+            raw = keep.tile([P, count, PACK, N], F32, name="w2_raw_%d" % first)
+            nc.sync.dma_start(
+                raw[:].rearrange("p e j n -> p e (j n)"),
+                w2[first:first + count].rearrange("e (p j) n -> p e (j n)", j=PACK),
+            )
+            return raw
+
+        def round_w1(raw, copy, name):
+            rounded = ring.tile([P, PACK * H], BF16, name=name, bufs=3, align_bytes=64)
+            copy(
+                rounded[:].rearrange("p (t m j) -> p m j t", t=PACK, j=PACK),
+                raw[:].rearrange("p j (m t) -> p m j t", t=PACK),
+            )
+            return rounded
+
+        def round_w2(raw, count, copy):
+            rounded = ring.tile([P, count * PACK * N], BF16, name="w2_bf16", bufs=4, align_bytes=64)
+            copy(
+                rounded[:].rearrange("p (e c i j) -> p e c j i", e=count, i=PACK, j=PACK),
+                raw[:].rearrange("p e j (c i) -> p e c j i", i=PACK),
+            )
+            return rounded
+
+        def quantize(rounded, width, name, bufs):
+            codes = ring.tile([P, width], U32, name=name + "_codes", bufs=bufs, align_bytes=64)
+            scales = ring.tile([P, width], U8, name=name + "_scales", bufs=bufs, align_bytes=64)
+            nc.vector.quantize_mx(out=codes[:].bitcast(FP8X4), scales=scales[:], in_=rounded[:, :])
+            return codes, scales
+
+        x_plane = keep.tile([P, T], U8, name="x_plane", align_bytes=64)
+        nc.vector.memset(x_plane[:].bitcast(I32), 0)
+        gate_rows = keep.tile([P, P], F32, name="gate_rows")
+        nc.vector.memset(gate_rows[:], 0.0)
+        zeros = keep.tile([P, PAD], F32, name="zeros")
+        nc.vector.memset(zeros[:], 0.0)
+        y = keep.tile([P, SLOTS + PAD], F32, name="y", align_bytes=64)
+        nc.scalar.activation(y[:, SLOTS:], zeros[:], RELU)
+        identity = keep.tile([P, P], F32, name="identity")
+        make_identity(nc, identity[:])
+
+        def load_x(o):
+            words = keep.tile([P, T], I32, name="x_words_%d" % o, align_bytes=64)
+            nc.sync.dma_start(words[:], x_words[o].rearrange("p t r -> p (t r)").bitcast(I32))
+            return words
+
+        x_tiles = [load_x(0)]
+        slot_tokens = load_list(offs, "slot_tokens")
+        x_tiles.append(load_x(1))
+        w1_raw = {(0, 0): load_w1(0, 0)}
+        for quadrant in range(4):
+            nc.sync.dma_start(
+                x_plane[32 * quadrant:32 * quadrant + 4 * PASSES, :].bitcast(I32),
+                x_scales[:, 4 * quadrant:4 * quadrant + 4, :].bitcast(I32),
+            )
+        w1_raw[0, 1] = load_w1(0, 1)
+
+        def gather_tokens(g):
+            offsets = slot_tokens[:, g * GATHER // PER_COLUMN:(g + 1) * GATHER // PER_COLUMN]
+            gathered = []
+            for o in range(PASSES):
+                words = ring.tile([P, GATHER], U32, name="slot_words_%d" % o, bufs=3, align_bytes=64)
+                nc.vector.tensor_copy(words[:], x_tiles[o][:].bitcast(U32).indirect(offsets))
+                gathered.append(words)
+            plane = ring.tile([P, GATHER], U8, name="slot_plane", bufs=3, align_bytes=64)
+            nc.vector.tensor_copy(plane[:], x_plane[:].indirect(offsets))
+            return gathered, plane
+
+        def first_layer(e, rounded, slots):
+            quantized = [quantize(rounded[o], H, "w1", 6) for o in range(PASSES)]
+            slot_words, slot_plane = slots
+            first = e * C % GATHER
+            cols = slice(first, first + C)
+            acc = psum.tile([P, PACK, C], F32, name="wide", bufs=4)
+            for t in range(PACK):
+                for o in range(PASSES):
+                    codes, scales = quantized[o]
+                    nc.tensor.matmul_mx(
+                        out=acc[:, t, :],
+                        lhsT=codes[:, t * P:(t + 1) * P].bitcast(FP8X4),
+                        lhsT_scale=scales[:, t * P:(t + 1) * P],
+                        rhs=slot_words[o][:, cols].bitcast(FP8X4),
+                        rhs_scale=slot_plane[4 * o:P, cols],
+                        start=(o == 0),
+                        stop=(o == PASSES - 1),
+                    )
+            return acc
+
+        def activate(acc, hidden):
+            nc.scalar.activation(
+                hidden.rearrange("p (c t) -> p c t", t=PACK),
+                acc[:].rearrange("p t c -> p c t"),
+                RELU,
+            )
+            return quantize(hidden, C, "hidden", E)
+
+        def second_layer(first, count, weights, acc):
+            codes, scales = weights
+            for i in range(count):
+                hidden_codes, hidden_scales = hidden_mx[first + i]
+                nc.tensor.matmul_mx(
+                    out=acc[:, i, :],
+                    lhsT=codes[:, i * N:(i + 1) * N].bitcast(FP8X4),
+                    lhsT_scale=scales[:, i * N:(i + 1) * N],
+                    rhs=hidden_codes[:].bitcast(FP8X4),
+                    rhs_scale=hidden_scales[:],
+                    start=True,
+                    stop=True,
+                )
+            nc.scalar.copy(y[:, first * C:(first + count) * C], acc[:, 0:count, :].rearrange("p e c -> p (e c)"))
+
+        def quantize_w2(raw, count, copy):
+            return quantize(round_w2(raw, count, copy), count * N, "w2", 4)
+
+        sources = (pos1, pos2, pos3, pos4)
+        token_slots = []
+        hidden_mx = []
+        sums_1 = []
+        w2_mx = {}
+        for e in range(E):
+            if e in W2_EARLY:
+                w2_raw = load_w2(*W2_EARLY[e])
+            if e + 1 < E:
+                for o in range(PASSES):
+                    w1_raw[e + 1, o] = load_w1(e + 1, o)
+            if e % 2 == 1 and e // 2 < TOP:
+                token_slots.append(load_list(sources[e // 2], "token_slots_%d" % (e // 2)))
+            if e == 2 * TOP:
+                nc.sync.dma_start(
+                    gate_rows[0:TOP * BLOCKS, :],
+                    gate[:, 0, :].rearrange("r (b t) -> r b t", t=P),
+                )
+                turned = psum.tile([P, P], F32, name="narrow", bufs=4)
+                nc.tensor.transpose(turned[:], gate_rows[:], identity[:])
+                gate_cols = keep.tile([P, TOP * BLOCKS], F32, name="gate_cols")
+                nc.scalar.copy(gate_cols[:], turned[:, 0:TOP * BLOCKS])
+            if e * C % GATHER == 0:
+                slots = gather_tokens(e * C // GATHER)
+            rounded = [
+                round_w1(w1_raw[e, 0], nc.scalar.copy, "w1_bf16_0"),
+                round_w1(w1_raw[e, 1], nc.vector.tensor_copy, "w1_bf16_1"),
+            ]
+            if e >= LAG:
+                spent = w1_raw[e, 0][:, 0, 0:PACK * C // 2].bitcast(BF16)
+                hidden_mx.append(activate(sums_1[e - LAG], spent))
+            if e - LAG - 1 in W2_EARLY:
+                second_layer(*W2_EARLY[e - LAG - 1], w2_mx[e - LAG - 1], sums_1[e - LAG])
+            sums_1.append(first_layer(e, rounded, slots))
+            if e in W2_EARLY:
+                w2_mx[e] = quantize_w2(w2_raw, W2_EARLY[e][1], nc.scalar.copy)
+        late_raw = [load_w2(*group) for group in W2_LATE]
+        for e in range(E - LAG, E):
+            last_hidden = keep.tile([P, PACK * C], BF16, name="hidden_%d" % e, align_bytes=64)
+            hidden_mx.append(activate(sums_1[e], last_hidden[:]))
+        for (first, count), raw in zip(W2_LATE, late_raw):
+            weights = quantize_w2(raw, count, nc.scalar.copy if count == 2 else nc.vector.tensor_copy)
+            acc = psum.tile([P, count, C], F32, name="narrow", bufs=4)
+            second_layer(first, count, weights, acc)
+
+        first = 0
+        for width in TOKEN_CHUNKS:
+            blocks = width // P
+            sums = [psum.tile([P, P], F32, name="narrow", bufs=4) for b in range(blocks)]
+            for r in range(TOP):
+                fetched = ring.tile([P, width], F32, name="fetched", bufs=4)
+                offsets = token_slots[r][:, first // PER_COLUMN:(first + width) // PER_COLUMN]
+                nc.vector.tensor_copy(fetched[:], y[:].indirect(offsets))
+                turned = psum.tile([P, blocks, P], F32, name="wide", bufs=4)
+                for b in range(blocks):
+                    nc.tensor.transpose(turned[:, b, :], fetched[:, b * P:(b + 1) * P], identity[:])
+                for b in range(blocks):
+                    col = r * BLOCKS + first // P + b
+                    gated = ring.tile([P, P], F32, name="gated", bufs=12)
+                    nc.scalar.activation(gated[:], turned[:, b, :], COPY, scale=gate_cols[:, col:col + 1])
+                    nc.tensor.matmul(
+                        sums[b][:], gated[:], identity[:],
+                        start=(r == 0), stop=(r == TOP - 1), is_transpose=True,
+                    )
+            result = ring.tile([P, width], F32, name="result", bufs=4)
+            for b in range(blocks):
+                nc.scalar.copy(result[:, b * P:(b + 1) * P], sums[b][:])
+            nc.sync.dma_start(out[:, first:first + width], result[:])
+            first = first + width

@@ -28,9 +28,11 @@ PER_COLUMN = 16
 GATHER = 256
 BLOCKS = T // P
 W2_EARLY = {1: (0, 2), 3: (2, 2), 5: (4, 2)}
+SCALAR_BOTH = (4, 8)
 LAG = 2
 W2_LATE = ((6, 2), (8, 2), (10, 1), (11, 1))
-TOKEN_CHUNKS = (512, 512, 256, 256)
+FIRST_CHUNKS = (512, 512)
+LAST_CHUNKS = (256, 256)
 
 
 def tile_moe_ecr_mlp_relu_kernel(
@@ -55,7 +57,7 @@ def tile_moe_ecr_mlp_relu_kernel(
             return raw
 
         def load_w2(first, count):
-            raw = keep.tile([P, count, PACK, N], F32, name="w2_raw_%d" % first)
+            raw = ring.tile([P, count, PACK, N], F32, name="w2_raw", bufs=5)
             nc.sync.dma_start(
                 raw[:].rearrange("p e j n -> p e (j n)"),
                 w2[first:first + count].rearrange("e (p j) n -> p e (j n)", j=PACK),
@@ -78,16 +80,20 @@ def tile_moe_ecr_mlp_relu_kernel(
             )
             return rounded
 
-        def quantize(rounded, width, name, bufs):
+        def quantize(rounded, width, name, bufs, pieces=1):
             codes = ring.tile([P, width], U32, name=name + "_codes", bufs=bufs, align_bytes=64)
             scales = ring.tile([P, width], U8, name=name + "_scales", bufs=bufs, align_bytes=64)
-            nc.vector.quantize_mx(out=codes[:].bitcast(FP8X4), scales=scales[:], in_=rounded[:, :])
+            step = width // pieces
+            for first in range(0, width, step):
+                nc.vector.quantize_mx(
+                    out=codes[:, first:first + step].bitcast(FP8X4),
+                    scales=scales[:, first:first + step],
+                    in_=rounded[:, PACK * first:PACK * (first + step)],
+                )
             return codes, scales
 
         x_plane = keep.tile([P, T], U8, name="x_plane", align_bytes=64)
         nc.vector.memset(x_plane[:].bitcast(I32), 0)
-        gate_rows = keep.tile([P, P], F32, name="gate_rows")
-        nc.vector.memset(gate_rows[:], 0.0)
         zeros = keep.tile([P, PAD], F32, name="zeros")
         nc.vector.memset(zeros[:], 0.0)
         y = keep.tile([P, SLOTS + PAD], F32, name="y", align_bytes=64)
@@ -123,7 +129,7 @@ def tile_moe_ecr_mlp_relu_kernel(
             return gathered, plane
 
         def first_layer(e, rounded, slots):
-            quantized = [quantize(rounded[o], H, "w1", 6) for o in range(PASSES)]
+            quantized = [quantize(rounded[o], H, "w1", 6, PACK if (e, o) == (E - 1, PASSES - 1) else 1) for o in range(PASSES)]
             slot_words, slot_plane = slots
             first = e * C % GATHER
             cols = slice(first, first + C)
@@ -181,22 +187,13 @@ def tile_moe_ecr_mlp_relu_kernel(
                     w1_raw[e + 1, o] = load_w1(e + 1, o)
             if e % 2 == 1 and e // 2 < TOP:
                 token_slots.append(load_list(sources[e // 2], "token_slots_%d" % (e // 2)))
-            if e == 2 * TOP:
-                nc.sync.dma_start(
-                    gate_rows[0:TOP * BLOCKS, :],
-                    gate[:, 0, :].rearrange("r (b t) -> r b t", t=P),
-                )
-                turned = psum.tile([P, P], F32, name="narrow", bufs=4)
-                nc.tensor.transpose(turned[:], gate_rows[:], identity[:])
-                gate_cols = keep.tile([P, TOP * BLOCKS], F32, name="gate_cols")
-                nc.scalar.copy(gate_cols[:], turned[:, 0:TOP * BLOCKS])
             if e * C % GATHER == 0:
                 slots = gather_tokens(e * C // GATHER)
             rounded = [
                 round_w1(w1_raw[e, 0], nc.scalar.copy, "w1_bf16_0"),
-                round_w1(w1_raw[e, 1], nc.vector.tensor_copy, "w1_bf16_1"),
+                round_w1(w1_raw[e, 1], nc.scalar.copy if e in SCALAR_BOTH else nc.vector.tensor_copy, "w1_bf16_1"),
             ]
-            if e >= LAG:
+            if LAG <= e < E - 1:
                 spent = w1_raw[e, 0][:, 0, 0:PACK * C // 2].bitcast(BF16)
                 hidden_mx.append(activate(sums_1[e - LAG], spent))
             if e - LAG - 1 in W2_EARLY:
@@ -205,7 +202,13 @@ def tile_moe_ecr_mlp_relu_kernel(
             if e in W2_EARLY:
                 w2_mx[e] = quantize_w2(w2_raw, W2_EARLY[e][1], nc.scalar.copy)
         late_raw = [load_w2(*group) for group in W2_LATE]
-        for e in range(E - LAG, E):
+        gates = {}
+        first = 0
+        for width in FIRST_CHUNKS + LAST_CHUNKS:
+            gates[first] = ring.tile([P, TOP, width], F32, name="w1_raw", bufs=10, align_bytes=64)
+            nc.sync.dma_start(gates[first][:], gate[:, :, first:first + width].rearrange("r n t -> n r t"))
+            first = first + width
+        for e in range(E - 1 - LAG, E):
             last_hidden = keep.tile([P, PACK * C], BF16, name="hidden_%d" % e, align_bytes=64)
             hidden_mx.append(activate(sums_1[e], last_hidden[:]))
         for (first, count), raw in zip(W2_LATE, late_raw):
@@ -213,27 +216,47 @@ def tile_moe_ecr_mlp_relu_kernel(
             acc = psum.tile([P, count, C], F32, name="narrow", bufs=4)
             second_layer(first, count, weights, acc)
 
-        first = 0
-        for width in TOKEN_CHUNKS:
-            blocks = width // P
-            sums = [psum.tile([P, P], F32, name="narrow", bufs=4) for b in range(blocks)]
-            for r in range(TOP):
-                fetched = ring.tile([P, width], F32, name="fetched", bufs=4)
-                offsets = token_slots[r][:, first // PER_COLUMN:(first + width) // PER_COLUMN]
-                nc.vector.tensor_copy(fetched[:], y[:].indirect(offsets))
-                turned = psum.tile([P, blocks, P], F32, name="wide", bufs=4)
-                for b in range(blocks):
-                    nc.tensor.transpose(turned[:, b, :], fetched[:, b * P:(b + 1) * P], identity[:])
-                for b in range(blocks):
-                    col = r * BLOCKS + first // P + b
-                    gated = ring.tile([P, P], F32, name="gated", bufs=12)
-                    nc.scalar.activation(gated[:], turned[:, b, :], COPY, scale=gate_cols[:, col:col + 1])
+        def fetch(products, r, first, width):
+            offsets = token_slots[r][:, first // PER_COLUMN:(first + width) // PER_COLUMN]
+            nc.vector.tensor_tensor(
+                products[:, r, :], y[:].indirect(offsets), gates[first][:, r, :], mybir.AluOpType.mult
+            )
+
+        def add_up(products, count, width):
+            turned = [psum.tile([P, P], F32, name="narrow", bufs=4) for b in range(width // P)]
+            for r in range(count):
+                for b, block in enumerate(turned):
                     nc.tensor.matmul(
-                        sums[b][:], gated[:], identity[:],
-                        start=(r == 0), stop=(r == TOP - 1), is_transpose=True,
+                        block[:], products[:, r, b * P:(b + 1) * P], identity[:],
+                        start=(r == 0), stop=(r == count - 1), is_transpose=True,
                     )
+            by_token = ring.tile([P, width], F32, name="by_token", bufs=2)
+            sums = psum.tile([P, width], F32, name="wide", bufs=4)
+            for b, block in enumerate(turned):
+                nc.scalar.copy(by_token[:, b * P:(b + 1) * P], block[:])
+                nc.tensor.transpose(sums[:, b * P:(b + 1) * P], by_token[:, b * P:(b + 1) * P], identity[:])
+            return sums
+
+        first = 0
+        for width in FIRST_CHUNKS:
+            products = ring.tile([P, TOP, width], F32, name="w1_raw", bufs=10, align_bytes=64)
+            for r in range(TOP):
+                fetch(products, r, first, width)
+            sums = add_up(products, TOP, width)
             result = ring.tile([P, width], F32, name="result", bufs=4)
-            for b in range(blocks):
-                nc.scalar.copy(result[:, b * P:(b + 1) * P], sums[b][:])
+            nc.scalar.copy(result[:], sums[:])
             nc.sync.dma_start(out[:, first:first + width], result[:])
             first = first + width
+        partial = []
+        for width in LAST_CHUNKS:
+            products = ring.tile([P, TOP, width], F32, name="w1_raw", bufs=10, align_bytes=64)
+            for r in range(TOP - 1):
+                fetch(products, r, first, width)
+            partial.append((first, width, products, add_up(products, TOP - 1, width)))
+            first = first + width
+        for first, width, products, sums in partial:
+            fetch(products, TOP - 1, first, width)
+        for first, width, products, sums in partial:
+            result = ring.tile([P, width], F32, name="result", bufs=4)
+            nc.vector.tensor_tensor(result[:], sums[:], products[:, TOP - 1, :], mybir.AluOpType.add)
+            nc.sync.dma_start(out[:, first:first + width], result[:])

@@ -27,12 +27,10 @@ PASSES = K // K_PASS
 PER_COLUMN = 16
 GATHER = 256
 BLOCKS = T // P
-W2_EARLY = {1: (0, 2), 3: (2, 2), 5: (4, 2)}
-SCALAR_BOTH = (4, 8)
+W2_EARLY = {2: (0, 2), 5: (2, 2)}
 LAG = 2
-W2_LATE = ((6, 2), (8, 2), (10, 1), (11, 1))
-FIRST_CHUNKS = (512, 512)
-LAST_CHUNKS = (256, 256)
+FIRST_CHUNKS = (512, 256)
+LAST_CHUNKS = (512, 256)
 
 
 def tile_moe_ecr_mlp_relu_kernel(
@@ -50,27 +48,26 @@ def tile_moe_ecr_mlp_relu_kernel(
             nc.sync.dma_start(tile[:], source)
             return tile
 
-        def load_w1(e, o):
-            raw = ring.tile([P, PACK, H], F32, name="w1_raw", bufs=10, align_bytes=64)
-            rows = w1[e, o * K_PASS:(o + 1) * K_PASS, :]
-            nc.sync.dma_start(raw[:], rows.rearrange("(p j) h -> p j h", j=PACK))
-            return raw
+        def stream_tile():
+            return ring.tile([P, 2, PACK, H], F32, name="stream", bufs=5, align_bytes=64)
+
+        def load_w1(e, raw, passes):
+            rows = w1[e].rearrange("(o p j) h -> p o (j h)", p=P, j=PACK)
+            nc.sync.dma_start(raw[:, passes].rearrange("p o j h -> p o (j h)"), rows[:, passes])
 
         def load_w2(first, count):
-            raw = ring.tile([P, count, PACK, N], F32, name="w2_raw", bufs=5)
+            raw = ring.tile([P, count, PACK, N], F32, name="w2_raw", bufs=5, align_bytes=64)
             nc.sync.dma_start(
                 raw[:].rearrange("p e j n -> p e (j n)"),
                 w2[first:first + count].rearrange("e (p j) n -> p e (j n)", j=PACK),
             )
             return raw
 
-        def round_w1(raw, copy, name):
-            rounded = ring.tile([P, PACK * H], BF16, name=name, bufs=3, align_bytes=64)
+        def round_w1(raw, rounded, copy):
             copy(
-                rounded[:].rearrange("p (t m j) -> p m j t", t=PACK, j=PACK),
-                raw[:].rearrange("p j (m t) -> p m j t", t=PACK),
+                rounded.rearrange("p (t m j) -> p m j t", t=PACK, j=PACK),
+                raw.rearrange("p j (m t) -> p m j t", t=PACK),
             )
-            return rounded
 
         def round_w2(raw, count, copy):
             rounded = ring.tile([P, count * PACK * N], BF16, name="w2_bf16", bufs=4, align_bytes=64)
@@ -107,15 +104,16 @@ def tile_moe_ecr_mlp_relu_kernel(
             return words
 
         x_tiles = [load_x(0)]
+        w1_raw = [stream_tile()]
+        load_w1(0, w1_raw[0], slice(0, 1))
         slot_tokens = load_list(offs, "slot_tokens")
-        x_tiles.append(load_x(1))
-        w1_raw = {(0, 0): load_w1(0, 0)}
         for quadrant in range(4):
             nc.sync.dma_start(
                 x_plane[32 * quadrant:32 * quadrant + 4 * PASSES, :].bitcast(I32),
                 x_scales[:, 4 * quadrant:4 * quadrant + 4, :].bitcast(I32),
             )
-        w1_raw[0, 1] = load_w1(0, 1)
+        x_tiles.append(load_x(1))
+        load_w1(0, w1_raw[0], slice(1, 2))
 
         def gather_tokens(g):
             offsets = slot_tokens[:, g * GATHER // PER_COLUMN:(g + 1) * GATHER // PER_COLUMN]
@@ -128,8 +126,7 @@ def tile_moe_ecr_mlp_relu_kernel(
             nc.vector.tensor_copy(plane[:], x_plane[:].indirect(offsets))
             return gathered, plane
 
-        def first_layer(e, rounded, slots):
-            quantized = [quantize(rounded[o], H, "w1", 6, PACK if (e, o) == (E - 1, PASSES - 1) else 1) for o in range(PASSES)]
+        def first_layer(e, quantized, slots):
             slot_words, slot_plane = slots
             first = e * C % GATHER
             cols = slice(first, first + C)
@@ -154,7 +151,6 @@ def tile_moe_ecr_mlp_relu_kernel(
                 acc[:].rearrange("p t c -> p c t"),
                 RELU,
             )
-            return quantize(hidden, C, "hidden", E)
 
         def second_layer(first, count, weights, acc):
             codes, scales = weights
@@ -169,13 +165,13 @@ def tile_moe_ecr_mlp_relu_kernel(
                     start=True,
                     stop=True,
                 )
-            nc.scalar.copy(y[:, first * C:(first + count) * C], acc[:, 0:count, :].rearrange("p e c -> p (e c)"))
+
+        def keep_results(first, count, acc, copy):
+            copy(y[:, first * C:(first + count) * C], acc[:, 0:count, :].rearrange("p e c -> p (e c)"))
 
         def quantize_w2(raw, count, copy):
-            return quantize(round_w2(raw, count, copy), count * N, "w2", 4)
+            return quantize(round_w2(raw, count, copy), count * N, "w2", 5)
 
-        sources = (pos1, pos2, pos3, pos4)
-        token_slots = []
         hidden_mx = []
         sums_1 = []
         w2_mx = {}
@@ -183,43 +179,87 @@ def tile_moe_ecr_mlp_relu_kernel(
             if e in W2_EARLY:
                 w2_raw = load_w2(*W2_EARLY[e])
             if e + 1 < E:
-                for o in range(PASSES):
-                    w1_raw[e + 1, o] = load_w1(e + 1, o)
-            if e % 2 == 1 and e // 2 < TOP:
-                token_slots.append(load_list(sources[e // 2], "token_slots_%d" % (e // 2)))
+                w1_raw.append(stream_tile())
+                load_w1(e + 1, w1_raw[e + 1], slice(0, 1))
+                if e + 2 == E:
+                    between_raw = load_w2(4, 2)
+                load_w1(e + 1, w1_raw[e + 1], slice(1, 2))
             if e * C % GATHER == 0:
                 slots = gather_tokens(e * C // GATHER)
-            rounded = [
-                round_w1(w1_raw[e, 0], nc.scalar.copy, "w1_bf16_0"),
-                round_w1(w1_raw[e, 1], nc.scalar.copy if e in SCALAR_BOTH else nc.vector.tensor_copy, "w1_bf16_1"),
-            ]
+            rounded = ring.tile([P, PASSES * PACK * H], BF16, name="w1_bf16", bufs=3, align_bytes=64)
+            halves = [rounded[:, o * PACK * H:(o + 1) * PACK * H] for o in range(PASSES)]
+            round_w1(w1_raw[e][:, 0], halves[0], nc.scalar.copy)
+            if e == E - 1:
+                between_mx = quantize_w2(between_raw, 2, nc.vector.tensor_copy)
+                quantized = [quantize(halves[0], H, "last", 1)]
+            round_w1(w1_raw[e][:, 1], halves[1], nc.vector.tensor_copy)
             if LAG <= e < E - 1:
-                spent = w1_raw[e, 0][:, 0, 0:PACK * C // 2].bitcast(BF16)
-                hidden_mx.append(activate(sums_1[e - LAG], spent))
+                spent = w1_raw[e][:, 0, 0, 0:PACK * C // 2].bitcast(BF16)
+                activate(sums_1[e - LAG], spent)
+                hidden_mx.append(quantize(spent, C, "hidden", E))
             if e - LAG - 1 in W2_EARLY:
-                second_layer(*W2_EARLY[e - LAG - 1], w2_mx[e - LAG - 1], sums_1[e - LAG])
-            sums_1.append(first_layer(e, rounded, slots))
+                first, count = W2_EARLY[e - LAG - 1]
+                second_layer(first, count, w2_mx[e - LAG - 1], sums_1[e - LAG])
+                keep_results(first, count, sums_1[e - LAG], nc.scalar.copy)
+            if e == E - 1:
+                quantized.append(quantize(halves[1], H, "w1", 3, PACK))
+            else:
+                codes, scales = quantize(rounded, PASSES * H, "w1", 3)
+                quantized = [(codes[:, o * H:(o + 1) * H], scales[:, o * H:(o + 1) * H]) for o in range(PASSES)]
+            sums_1.append(first_layer(e, quantized, slots))
             if e in W2_EARLY:
                 w2_mx[e] = quantize_w2(w2_raw, W2_EARLY[e][1], nc.scalar.copy)
-        late_raw = [load_w2(*group) for group in W2_LATE]
-        gates = {}
+        late_raw = [load_w2(*group) for group in ((6, 2), (8, 2), (10, 1), (11, 1))]
+
+        token_slots = []
+        staged = {}
+        by_row = gate.rearrange("r n t -> n r t")
+
+        def load_gates(first, width, choices):
+            nc.sync.dma_start(staged[first][:, 0, choices, 0:width], by_row[:, choices, first:first + width])
+
         first = 0
         for width in FIRST_CHUNKS + LAST_CHUNKS:
-            gates[first] = ring.tile([P, TOP, width], F32, name="w1_raw", bufs=10, align_bytes=64)
-            nc.sync.dma_start(gates[first][:], gate[:, :, first:first + width].rearrange("r n t -> n r t"))
+            staged[first] = stream_tile()
+            if first == 0:
+                for r, source in enumerate((pos1, pos2, pos3, pos4)):
+                    token_slots.append(load_list(source, "token_slots_%d" % r))
+                    load_gates(first, width, slice(r, r + 1))
+            else:
+                load_gates(first, width, slice(0, TOP if first < sum(FIRST_CHUNKS) else TOP - 1))
             first = first + width
-        for e in range(E - 1 - LAG, E):
-            last_hidden = keep.tile([P, PACK * C], BF16, name="hidden_%d" % e, align_bytes=64)
-            hidden_mx.append(activate(sums_1[e], last_hidden[:]))
-        for (first, count), raw in zip(W2_LATE, late_raw):
-            weights = quantize_w2(raw, count, nc.scalar.copy if count == 2 else nc.vector.tensor_copy)
-            acc = psum.tile([P, count, C], F32, name="narrow", bufs=4)
-            second_layer(first, count, weights, acc)
+        first = sum(FIRST_CHUNKS)
+        for width in LAST_CHUNKS:
+            load_gates(first, width, slice(TOP - 1, TOP))
+            first = first + width
+
+        spent = w1_raw[E - 1][:, 0, 0, :].bitcast(BF16)
+        for i in range(LAG):
+            activate(sums_1[E - 1 - LAG + i], spent[:, i * PACK * C:(i + 1) * PACK * C])
+        codes, scales = quantize(spent, LAG * C, "last", 1)
+        hidden_mx.extend((codes[:, i * C:(i + 1) * C], scales[:, i * C:(i + 1) * C]) for i in range(LAG))
+        acc = psum.tile([P, 2, C], F32, name="narrow", bufs=4)
+        second_layer(4, 2, between_mx, acc)
+        keep_results(4, 2, acc, nc.scalar.copy)
+        late_mx = [quantize_w2(raw, 2, nc.scalar.copy) for raw in late_raw[:2]]
+        late_mx.extend(quantize_w2(raw, 1, nc.vector.tensor_copy) for raw in late_raw[2:])
+        spent = late_raw[1][:, 0].rearrange("p j n -> p (j n)")[:, 0:PACK * C // 2].bitcast(BF16)
+        activate(sums_1[E - 1], spent)
+        hidden_mx.append(quantize(spent, C, "hidden", E))
+        second_layer(6, 2, late_mx[0], sums_1[E - 1])
+        keep_results(6, 2, sums_1[E - 1], nc.scalar.copy)
+        acc = psum.tile([P, 3, C], F32, name="narrow", bufs=4)
+        second_layer(8, 2, late_mx[1], acc[:, 0:2])
+        second_layer(10, 1, late_mx[2], acc[:, 2:3])
+        keep_results(8, 3, acc, nc.scalar.copy)
+        acc = psum.tile([P, 1, C], F32, name="narrow", bufs=4)
+        second_layer(11, 1, late_mx[3], acc)
+        keep_results(11, 1, acc, nc.vector.tensor_copy)
 
         def fetch(products, r, first, width):
             offsets = token_slots[r][:, first // PER_COLUMN:(first + width) // PER_COLUMN]
             nc.vector.tensor_tensor(
-                products[:, r, :], y[:].indirect(offsets), gates[first][:, r, :], mybir.AluOpType.mult
+                products[:, r, :], y[:].indirect(offsets), staged[first][:, 0, r, 0:width], mybir.AluOpType.mult
             )
 
         def add_up(products, count, width):
@@ -239,7 +279,7 @@ def tile_moe_ecr_mlp_relu_kernel(
 
         first = 0
         for width in FIRST_CHUNKS:
-            products = ring.tile([P, TOP, width], F32, name="w1_raw", bufs=10, align_bytes=64)
+            products = staged[first][:, 1, :, 0:width]
             for r in range(TOP):
                 fetch(products, r, first, width)
             sums = add_up(products, TOP, width)
@@ -249,7 +289,7 @@ def tile_moe_ecr_mlp_relu_kernel(
             first = first + width
         partial = []
         for width in LAST_CHUNKS:
-            products = ring.tile([P, TOP, width], F32, name="w1_raw", bufs=10, align_bytes=64)
+            products = staged[first][:, 1, :, 0:width]
             for r in range(TOP - 1):
                 fetch(products, r, first, width)
             partial.append((first, width, products, add_up(products, TOP - 1, width)))

@@ -29,6 +29,7 @@ GATHER = 256
 BLOCKS = T // P
 W2_EARLY = {2: (0, 2), 5: (2, 2)}
 LAG = 2
+SPLIT = 3
 FIRST_CHUNKS = (512, 256)
 LAST_CHUNKS = (512, 256)
 
@@ -56,7 +57,7 @@ def tile_moe_ecr_mlp_relu_kernel(
             nc.sync.dma_start(raw[:, passes].rearrange("p o j h -> p o (j h)"), rows[:, passes])
 
         def load_w2(first, count):
-            raw = ring.tile([P, count, PACK, N], F32, name="w2_raw", bufs=5, align_bytes=64)
+            raw = ring.tile([P, count, PACK, N], F32, name="w2_raw", bufs=6, align_bytes=64)
             nc.sync.dma_start(
                 raw[:].rearrange("p e j n -> p e (j n)"),
                 w2[first:first + count].rearrange("e (p j) n -> p e (j n)", j=PACK),
@@ -70,7 +71,7 @@ def tile_moe_ecr_mlp_relu_kernel(
             )
 
         def round_w2(raw, count, copy):
-            rounded = ring.tile([P, count * PACK * N], BF16, name="w2_bf16", bufs=4, align_bytes=64)
+            rounded = ring.tile([P, count * PACK * N], BF16, name="w2_bf16", bufs=5, align_bytes=64)
             copy(
                 rounded[:].rearrange("p (e c i j) -> p e c j i", e=count, i=PACK, j=PACK),
                 raw[:].rearrange("p e j (c i) -> p e c j i", i=PACK),
@@ -103,17 +104,21 @@ def tile_moe_ecr_mlp_relu_kernel(
             nc.sync.dma_start(words[:], x_words[o].rearrange("p t r -> p (t r)").bitcast(I32))
             return words
 
+        def load_scale_rows(o):
+            for quadrant in range(4):
+                row = 32 * quadrant + 4 * o
+                nc.sync.dma_start(
+                    x_plane[row:row + 4, :].bitcast(I32),
+                    x_scales[o, 4 * quadrant:4 * quadrant + 4, :].bitcast(I32),
+                )
+
         x_tiles = [load_x(0)]
-        w1_raw = [stream_tile()]
-        load_w1(0, w1_raw[0], slice(0, 1))
         slot_tokens = load_list(offs, "slot_tokens")
-        for quadrant in range(4):
-            nc.sync.dma_start(
-                x_plane[32 * quadrant:32 * quadrant + 4 * PASSES, :].bitcast(I32),
-                x_scales[:, 4 * quadrant:4 * quadrant + 4, :].bitcast(I32),
-            )
+        load_scale_rows(0)
         x_tiles.append(load_x(1))
-        load_w1(0, w1_raw[0], slice(1, 2))
+        w1_raw = [stream_tile()]
+        load_w1(0, w1_raw[0], slice(0, PASSES))
+        load_scale_rows(1)
 
         def gather_tokens(g):
             offsets = slot_tokens[:, g * GATHER // PER_COLUMN:(g + 1) * GATHER // PER_COLUMN]
@@ -170,8 +175,9 @@ def tile_moe_ecr_mlp_relu_kernel(
             copy(y[:, first * C:(first + count) * C], acc[:, 0:count, :].rearrange("p e c -> p (e c)"))
 
         def quantize_w2(raw, count, copy):
-            return quantize(round_w2(raw, count, copy), count * N, "w2", 5)
+            return quantize(round_w2(raw, count, copy), count * N, "w2", 6)
 
+        late = ((6, 2, nc.scalar.copy), (8, 2, nc.scalar.copy), (10, 1, nc.vector.tensor_copy), (11, 1, nc.vector.tensor_copy))
         hidden_mx = []
         sums_1 = []
         w2_mx = {}
@@ -180,6 +186,9 @@ def tile_moe_ecr_mlp_relu_kernel(
                 w2_raw = load_w2(*W2_EARLY[e])
             if e + 1 < E:
                 w1_raw.append(stream_tile())
+            if e + 1 < E - SPLIT:
+                load_w1(e + 1, w1_raw[e + 1], slice(0, PASSES))
+            if E - SPLIT <= e + 1 < E:
                 load_w1(e + 1, w1_raw[e + 1], slice(0, 1))
                 if e + 2 == E:
                     between_raw = load_w2(4, 2)
@@ -209,7 +218,7 @@ def tile_moe_ecr_mlp_relu_kernel(
             sums_1.append(first_layer(e, quantized, slots))
             if e in W2_EARLY:
                 w2_mx[e] = quantize_w2(w2_raw, W2_EARLY[e][1], nc.scalar.copy)
-        late_raw = [load_w2(*group) for group in ((6, 2), (8, 2), (10, 1), (11, 1))]
+        late_raw = [load_w2(first, count) for first, count, copy in late]
 
         token_slots = []
         staged = {}
@@ -241,19 +250,19 @@ def tile_moe_ecr_mlp_relu_kernel(
         acc = psum.tile([P, 2, C], F32, name="narrow", bufs=4)
         second_layer(4, 2, between_mx, acc)
         keep_results(4, 2, acc, nc.scalar.copy)
-        late_mx = [quantize_w2(raw, 2, nc.scalar.copy) for raw in late_raw[:2]]
-        late_mx.extend(quantize_w2(raw, 1, nc.vector.tensor_copy) for raw in late_raw[2:])
+        late_mx = [quantize_w2(raw, count, copy) for (first, count, copy), raw in zip(late, late_raw)]
         spent = late_raw[1][:, 0].rearrange("p j n -> p (j n)")[:, 0:PACK * C // 2].bitcast(BF16)
         activate(sums_1[E - 1], spent)
         hidden_mx.append(quantize(spent, C, "hidden", E))
-        second_layer(6, 2, late_mx[0], sums_1[E - 1])
-        keep_results(6, 2, sums_1[E - 1], nc.scalar.copy)
+        acc = sums_1[E - 1]
+        second_layer(6, 2, late_mx[0], acc[:, 0:2])
+        keep_results(6, 2, acc, nc.vector.tensor_copy)
         acc = psum.tile([P, 3, C], F32, name="narrow", bufs=4)
         second_layer(8, 2, late_mx[1], acc[:, 0:2])
         second_layer(10, 1, late_mx[2], acc[:, 2:3])
         keep_results(8, 3, acc, nc.scalar.copy)
         acc = psum.tile([P, 1, C], F32, name="narrow", bufs=4)
-        second_layer(11, 1, late_mx[3], acc)
+        second_layer(11, 1, late_mx[3], acc[:, 0:1])
         keep_results(11, 1, acc, nc.vector.tensor_copy)
 
         def fetch(products, r, first, width):
@@ -296,7 +305,6 @@ def tile_moe_ecr_mlp_relu_kernel(
             first = first + width
         for first, width, products, sums in partial:
             fetch(products, TOP - 1, first, width)
-        for first, width, products, sums in partial:
             result = ring.tile([P, width], F32, name="result", bufs=4)
             nc.vector.tensor_tensor(result[:], sums[:], products[:, TOP - 1, :], mybir.AluOpType.add)
             nc.sync.dma_start(out[:, first:first + width], result[:])

from contextlib import ExitStack

import concourse.mybir as mybir
from concourse.masks import make_identity

K, T, E, C, H, N = 1024, 1536, 12, 128, 512, 128
TOP = 4
PAD = 64
SLOTS = E * C

FLOPS = 2 * SLOTS * (K * H + H * N)

F32 = mybir.dt.float32
BF16 = mybir.dt.bfloat16
I32 = mybir.dt.int32
U32 = mybir.dt.uint32
U16 = mybir.dt.uint16
U8 = mybir.dt.uint8
FP8X4 = mybir.dt.float8_e4m3fn_x4
RELU = mybir.ActivationFunctionType.Relu
COPY = mybir.ActivationFunctionType.Copy

P = 128
PACK = 4
K_PASS = P * PACK
PASSES = K // K_PASS
PER_COLUMN = 16
GATHER = 256
BLOCKS = T // P
W2_EARLY = {2: (0, 2), 5: (2, 2)}
LAG = 2
SPLIT = 3
FIRST_CHUNKS = (512, 256)
LAST_CHUNKS = (512, 256)


def tile_moe_ecr_mlp_relu_kernel(
    tc, x_words, x_scales, w1, w2, gate, offs, pos1, pos2, pos3, pos4, out
):
    nc = tc.nc
    with ExitStack() as ctx:
        lists = ctx.enter_context(tc.tile_pool(name="lists", bufs=1))
        keep = ctx.enter_context(tc.tile_pool(name="keep", bufs=1))
        ring = ctx.enter_context(tc.tile_pool(name="ring", bufs=1))
        psum = ctx.enter_context(tc.psum_pool(name="psum", bufs=1))

        def load_list(source, name):
            tile = lists.tile([P, T // PER_COLUMN], U16, name=name)
            nc.sync.dma_start(tile[:], source)
            return tile

        def stream_tile():
            return ring.tile([P, 2, PACK, H], F32, name="stream", bufs=5, align_bytes=64)

        def load_w1(e, raw, passes):
            rows = w1[e].rearrange("(o p j) h -> p o (j h)", p=P, j=PACK)
            nc.sync.dma_start(raw[:, passes].rearrange("p o j h -> p o (j h)"), rows[:, passes])

        def load_w2(first, count):
            raw = ring.tile([P, count, PACK, N], F32, name="w2_raw", bufs=6, align_bytes=64)
            nc.sync.dma_start(
                raw[:].rearrange("p e j n -> p e (j n)"),
                w2[first:first + count].rearrange("e (p j) n -> p e (j n)", j=PACK),
            )
            return raw

        def round_w1(raw, rounded, copy):
            copy(
                rounded.rearrange("p (t m j) -> p m j t", t=PACK, j=PACK),
                raw.rearrange("p j (m t) -> p m j t", t=PACK),
            )

        def round_w2(raw, count, copy):
            rounded = ring.tile([P, count * PACK * N], BF16, name="w2_bf16", bufs=5, align_bytes=64)
            copy(
                rounded[:].rearrange("p (e c i j) -> p e c j i", e=count, i=PACK, j=PACK),
                raw[:].rearrange("p e j (c i) -> p e c j i", i=PACK),
            )
            return rounded

        def quantize(rounded, width, name, bufs, pieces=1):
            codes = ring.tile([P, width], U32, name=name + "_codes", bufs=bufs, align_bytes=64)
            scales = ring.tile([P, width], U8, name=name + "_scales", bufs=bufs, align_bytes=64)
            step = width // pieces
            for first in range(0, width, step):
                nc.vector.quantize_mx(
                    out=codes[:, first:first + step].bitcast(FP8X4),
                    scales=scales[:, first:first + step],
                    in_=rounded[:, PACK * first:PACK * (first + step)],
                )
            return codes, scales

        x_plane = keep.tile([P, T], U8, name="x_plane", align_bytes=64)
        nc.vector.memset(x_plane[:].bitcast(I32), 0)
        zeros = keep.tile([P, PAD], F32, name="zeros")
        nc.vector.memset(zeros[:], 0.0)
        y = keep.tile([P, SLOTS + PAD], F32, name="y", align_bytes=64)
        nc.scalar.activation(y[:, SLOTS:], zeros[:], RELU)
        identity = keep.tile([P, P], F32, name="identity")
        make_identity(nc, identity[:])

        def load_x(o):
            words = keep.tile([P, T], I32, name="x_words_%d" % o, align_bytes=64)
            nc.sync.dma_start(words[:], x_words[o].rearrange("p t r -> p (t r)").bitcast(I32))
            return words

        def load_scale_rows(o):
            for quadrant in range(4):
                row = 32 * quadrant + 4 * o
                nc.sync.dma_start(
                    x_plane[row:row + 4, :].bitcast(I32),
                    x_scales[o, 4 * quadrant:4 * quadrant + 4, :].bitcast(I32),
                )

        x_tiles = [load_x(0)]
        slot_tokens = load_list(offs, "slot_tokens")
        load_scale_rows(0)
        x_tiles.append(load_x(1))
        w1_raw = [stream_tile()]
        load_w1(0, w1_raw[0], slice(0, PASSES))
        load_scale_rows(1)

        def gather_tokens(g):
            offsets = slot_tokens[:, g * GATHER // PER_COLUMN:(g + 1) * GATHER // PER_COLUMN]
            gathered = []
            for o in range(PASSES):
                words = ring.tile([P, GATHER], U32, name="slot_words_%d" % o, bufs=3, align_bytes=64)
                nc.vector.tensor_copy(words[:], x_tiles[o][:].bitcast(U32).indirect(offsets))
                gathered.append(words)
            plane = ring.tile([P, GATHER], U8, name="slot_plane", bufs=3, align_bytes=64)
            nc.vector.tensor_copy(plane[:], x_plane[:].indirect(offsets))
            return gathered, plane

        def first_layer(e, quantized, slots):
            slot_words, slot_plane = slots
            first = e * C % GATHER
            cols = slice(first, first + C)
            acc = psum.tile([P, PACK, C], F32, name="wide", bufs=4)
            for t in range(PACK):
                for o in range(PASSES):
                    codes, scales = quantized[o]
                    nc.tensor.matmul_mx(
                        out=acc[:, t, :],
                        lhsT=codes[:, t * P:(t + 1) * P].bitcast(FP8X4),
                        lhsT_scale=scales[:, t * P:(t + 1) * P],
                        rhs=slot_words[o][:, cols].bitcast(FP8X4),
                        rhs_scale=slot_plane[4 * o:P, cols],
                        start=(o == 0),
                        stop=(o == PASSES - 1),
                    )
            return acc

        def activate(acc, hidden):
            nc.scalar.activation(
                hidden.rearrange("p (c t) -> p c t", t=PACK),
                acc[:].rearrange("p t c -> p c t"),
                RELU,
            )

        def second_layer(first, count, weights, acc):
            codes, scales = weights
            for i in range(count):
                hidden_codes, hidden_scales = hidden_mx[first + i]
                nc.tensor.matmul_mx(
                    out=acc[:, i, :],
                    lhsT=codes[:, i * N:(i + 1) * N].bitcast(FP8X4),
                    lhsT_scale=scales[:, i * N:(i + 1) * N],
                    rhs=hidden_codes[:].bitcast(FP8X4),
                    rhs_scale=hidden_scales[:],
                    start=True,
                    stop=True,
                )

        def keep_results(first, count, acc, copy):
            copy(y[:, first * C:(first + count) * C], acc[:, 0:count, :].rearrange("p e c -> p (e c)"))

        def quantize_w2(raw, count, copy):
            return quantize(round_w2(raw, count, copy), count * N, "w2", 6)

        late = ((6, 2, nc.scalar.copy), (8, 2, nc.scalar.copy), (10, 1, nc.vector.tensor_copy), (11, 1, nc.vector.tensor_copy))
        hidden_mx = []
        sums_1 = []
        w2_mx = {}
        for e in range(E):
            if e in W2_EARLY:
                w2_raw = load_w2(*W2_EARLY[e])
            if e + 1 < E:
                w1_raw.append(stream_tile())
            if e + 1 < E - SPLIT:
                load_w1(e + 1, w1_raw[e + 1], slice(0, PASSES))
            if E - SPLIT <= e + 1 < E:
                load_w1(e + 1, w1_raw[e + 1], slice(0, 1))
                if e + 2 == E:
                    between_raw = load_w2(4, 2)
                load_w1(e + 1, w1_raw[e + 1], slice(1, 2))
            if e * C % GATHER == 0:
                slots = gather_tokens(e * C // GATHER)
            rounded = ring.tile([P, PASSES * PACK * H], BF16, name="w1_bf16", bufs=3, align_bytes=64)
            halves = [rounded[:, o * PACK * H:(o + 1) * PACK * H] for o in range(PASSES)]
            round_w1(w1_raw[e][:, 0], halves[0], nc.scalar.copy)
            if e == E - 1:
                between_mx = quantize_w2(between_raw, 2, nc.vector.tensor_copy)
                quantized = [quantize(halves[0], H, "last", 1)]
            round_w1(w1_raw[e][:, 1], halves[1], nc.vector.tensor_copy)
            if LAG <= e < E - 1:
                spent = w1_raw[e][:, 0, 0, 0:PACK * C // 2].bitcast(BF16)
                activate(sums_1[e - LAG], spent)
                hidden_mx.append(quantize(spent, C, "hidden", E))
            if e - LAG - 1 in W2_EARLY:
                first, count = W2_EARLY[e - LAG - 1]
                second_layer(first, count, w2_mx[e - LAG - 1], sums_1[e - LAG])
                keep_results(first, count, sums_1[e - LAG], nc.scalar.copy)
            if e == E - 1:
                quantized.append(quantize(halves[1], H, "w1", 3, PACK))
            else:
                codes, scales = quantize(rounded, PASSES * H, "w1", 3)
                quantized = [(codes[:, o * H:(o + 1) * H], scales[:, o * H:(o + 1) * H]) for o in range(PASSES)]
            sums_1.append(first_layer(e, quantized, slots))
            if e in W2_EARLY:
                w2_mx[e] = quantize_w2(w2_raw, W2_EARLY[e][1], nc.scalar.copy)
        late_raw = [load_w2(first, count) for first, count, copy in late]

        token_slots = []
        staged = {}
        by_row = gate.rearrange("r n t -> n r t")

        def load_gates(first, width, choices):
            nc.sync.dma_start(staged[first][:, 0, choices, 0:width], by_row[:, choices, first:first + width])

        first = 0
        for width in FIRST_CHUNKS + LAST_CHUNKS:
            staged[first] = stream_tile()
            if first == 0:
                for r, source in enumerate((pos1, pos2, pos3, pos4)):
                    token_slots.append(load_list(source, "token_slots_%d" % r))
                    load_gates(first, width, slice(r, r + 1))
            else:
                load_gates(first, width, slice(0, TOP if first < sum(FIRST_CHUNKS) else TOP - 1))
            first = first + width
        first = sum(FIRST_CHUNKS)
        for width in LAST_CHUNKS:
            load_gates(first, width, slice(TOP - 1, TOP))
            first = first + width

        spent = w1_raw[E - 1][:, 0, 0, :].bitcast(BF16)
        for i in range(LAG):
            activate(sums_1[E - 1 - LAG + i], spent[:, i * PACK * C:(i + 1) * PACK * C])
        codes, scales = quantize(spent, LAG * C, "last", 1)
        hidden_mx.extend((codes[:, i * C:(i + 1) * C], scales[:, i * C:(i + 1) * C]) for i in range(LAG))
        acc = psum.tile([P, 2, C], F32, name="narrow", bufs=4)
        second_layer(4, 2, between_mx, acc)
        keep_results(4, 2, acc, nc.scalar.copy)
        late_mx = [quantize_w2(raw, count, copy) for (first, count, copy), raw in zip(late, late_raw)]
        spent = late_raw[1][:, 0].rearrange("p j n -> p (j n)")[:, 0:PACK * C // 2].bitcast(BF16)
        activate(sums_1[E - 1], spent)
        hidden_mx.append(quantize(spent, C, "hidden", E))
        acc = sums_1[E - 1]
        second_layer(6, 2, late_mx[0], acc[:, 0:2])
        keep_results(6, 2, acc, nc.vector.tensor_copy)
        acc = psum.tile([P, 3, C], F32, name="narrow", bufs=4)
        second_layer(8, 2, late_mx[1], acc[:, 0:2])
        second_layer(10, 1, late_mx[2], acc[:, 2:3])
        keep_results(8, 3, acc, nc.scalar.copy)
        acc = psum.tile([P, 1, C], F32, name="narrow", bufs=4)
        second_layer(11, 1, late_mx[3], acc[:, 0:1])
        keep_results(11, 1, acc, nc.vector.tensor_copy)

        def fetch(products, r, first, width):
            offsets = token_slots[r][:, first // PER_COLUMN:(first + width) // PER_COLUMN]
            nc.vector.tensor_tensor(
                products[:, r, :], y[:].indirect(offsets), staged[first][:, 0, r, 0:width], mybir.AluOpType.mult
            )

        def add_up(products, count, width):
            turned = [psum.tile([P, P], F32, name="narrow", bufs=4) for b in range(width // P)]
            for r in range(count):
                for b, block in enumerate(turned):
                    nc.tensor.matmul(
                        block[:], products[:, r, b * P:(b + 1) * P], identity[:],
                        start=(r == 0), stop=(r == count - 1), is_transpose=True,
                    )
            by_token = ring.tile([P, width], F32, name="by_token", bufs=2)
            sums = psum.tile([P, width], F32, name="wide", bufs=4)
            for b, block in enumerate(turned):
                nc.scalar.copy(by_token[:, b * P:(b + 1) * P], block[:])
                nc.tensor.transpose(sums[:, b * P:(b + 1) * P], by_token[:, b * P:(b + 1) * P], identity[:])
            return sums

        first = 0
        for width in FIRST_CHUNKS:
            products = staged[first][:, 1, :, 0:width]
            for r in range(TOP):
                fetch(products, r, first, width)
            sums = add_up(products, TOP, width)
            result = ring.tile([P, width], F32, name="result", bufs=4)
            nc.scalar.copy(result[:], sums[:])
            nc.sync.dma_start(out[:, first:first + width], result[:])
            first = first + width
        partial = []
        for width in LAST_CHUNKS:
            products = staged[first][:, 1, :, 0:width]
            for r in range(TOP - 1):
                fetch(products, r, first, width)
            partial.append((first, width, products, add_up(products, TOP - 1, width)))
            first = first + width
        for first, width, products, sums in partial:
            fetch(products, TOP - 1, first, width)
            result = ring.tile([P, width], F32, name="result", bufs=4)
            nc.vector.tensor_tensor(result[:], sums[:], products[:, TOP - 1, :], mybir.AluOpType.add)
            nc.sync.dma_start(out[:, first:first + width], result[:])
